import numpy as np
import ml_dtypes


def mxq(x, axis, fmt="e4m3"):
    dtype, down = {"e4m3": (ml_dtypes.float8_e4m3fn, 7), "e5m2": (ml_dtypes.float8_e5m2, 14)}[fmt]
    v = np.moveaxis(np.asarray(x, np.float32).astype(ml_dtypes.bfloat16).astype(np.float64), axis, -1)
    blocks = v.reshape(v.shape[:-1] + (-1, 32))
    amax = np.abs(blocks).max(-1, keepdims=True)
    byte = np.maximum(np.where(amax > 0, np.frexp(amax)[1] - 1 + 127, 0) - down, 1)
    scale = np.exp2(byte - 127.0)
    codes = (blocks / scale).astype(np.float32).astype(dtype).astype(np.float64)
    return np.moveaxis((codes * scale).reshape(v.shape), -1, axis)


WIDE = False


def mx_kscale(k, group=512):
    if not WIDE:
        return np.ones(k)
    levels = np.array([10, -10, 5, -5, 0])
    if group != 512:
        return np.exp2(np.random.permutation(np.resize(levels, k // group))).repeat(group)
    if k % 512:
        return np.exp2(np.random.permutation(np.resize(levels, k // 32))).repeat(32)
    a = np.empty((k // 512, 16))
    for p in range(k // 512):
        a[p, :8] = np.random.permutation(np.resize(levels, 8))
        for g in range(8):
            far = levels[np.abs(levels - a[p, g]) >= 10]
            a[p, g + 8] = far[np.random.randint(len(far))]
    return np.exp2(a.ravel()).repeat(32)


def f64(x):
    return np.asarray(x).astype(np.float64)


E2M1 = np.array([0.0, 0.5, 1.0, 1.5, 2.0, 3.0, 4.0, 6.0, -0.0, -0.5, -1.0, -1.5, -2.0, -3.0, -4.0, -6.0])


def pack_group(w):
    k, n = w.shape
    w = f64(np.asarray(w, np.float32).astype(ml_dtypes.bfloat16)).reshape(k // 32, 32, n)
    amax = np.abs(w).max(1)
    mant, ex = np.frexp(amax / 6.0)
    byte = np.clip(np.where(amax > 0, np.where(mant > 0.5, ex, ex - 1) + 127, 1), 1, 254)
    scaled = (w * np.exp2(127.0 - byte)[:, None, :]).reshape(k, n).astype(np.float32)
    c = np.ascontiguousarray(scaled.reshape(k // 4, 4, n).transpose(0, 2, 1)).astype(ml_dtypes.float4_e2m1fn).view(np.uint8) & 0xF
    return np.ascontiguousarray((c[..., 0::2] | (c[..., 1::2] << 4)).reshape(k // 4, 2 * n)), byte.astype(np.uint8)


def unpack_group(words, scales):
    p, n = words.shape[0], scales.shape[1]
    words = np.ascontiguousarray(words).reshape(p, n, 2)
    nib = np.empty((p, n, 4), np.uint8)
    nib[..., 0::2] = words & 0xF
    nib[..., 1::2] = words >> 4
    return E2M1[nib].transpose(0, 2, 1).reshape(4 * p, n) * np.repeat(np.exp2(scales.astype(np.float64) - 127.0), 32, axis=0)


def silu(v):
    return v / (1.0 + np.exp(-v))


def sigmoid(v):
    return 1.0 / (1.0 + np.exp(-v))


G, D, M, O, N = 2, 256, 256, 256, 512


def setup_inputs():
    n = np.random.standard_normal
    s_d = mx_kscale(D, 0)
    s_o = mx_kscale(O, 0)
    w1_ = [pack_group(w) for w in n((G, D, M)) / np.sqrt(D) / s_d[:, None]]
    w2_ = [pack_group(w) for w in n((G, D, M)) / np.sqrt(D) / s_d[:, None]]
    w3_ = [pack_group(w) for w in n((G, D, M)) / np.sqrt(D) / s_d[:, None]]
    wo_ = [pack_group(w) for w in n((G, O, M)) / np.sqrt(O) / s_o[:, None]]
    return {
        "x": (n((G, D, N)) * s_d[:, None]).astype(np.float32),
        "w1_words": np.stack([w[0] for w in w1_]),
        "w1_scales": np.stack([w[1] for w in w1_]),
        "w2_words": np.stack([w[0] for w in w2_]),
        "w2_scales": np.stack([w[1] for w in w2_]),
        "w3_words": np.stack([w[0] for w in w3_]),
        "w3_scales": np.stack([w[1] for w in w3_]),
        "b3": (0.5 * n((G, M, 1))).astype(np.float32),
        "wo_words": np.stack([w[0] for w in wo_]),
        "wo_scales": np.stack([w[1] for w in wo_]),
        "dy": (n((G, O, N)) * s_o[:, None]).astype(np.float32),
        "old": (0.3 * n((G, M, N))).astype(np.float32),
    }


def reference(x, w1_words, w1_scales, w2_words, w2_scales, w3_words, w3_scales, b3, wo_words, wo_scales, dy, old):
    w1 = np.stack([unpack_group(w1_words[g], w1_scales[g]) for g in range(G)])
    xq = mxq(f64(x), 1, "e4m3")
    z1 = w1.transpose(0, 2, 1) @ xq
    w2 = np.stack([unpack_group(w2_words[g], w2_scales[g]) for g in range(G)])
    z2 = w2.transpose(0, 2, 1) @ xq
    w3 = np.stack([unpack_group(w3_words[g], w3_scales[g]) for g in range(G)])
    z3 = w3.transpose(0, 2, 1) @ xq
    e1 = np.tanh(z1)
    e2 = silu(z2)
    gt = sigmoid(z3 + f64(b3))
    wo = np.stack([unpack_group(wo_words[g], wo_scales[g]) for g in range(G)])
    dyq = mxq(f64(dy), 1, "e4m3")
    c0 = wo.transpose(0, 2, 1) @ dyq
    dgt = c0 * (e1 - e2)
    dz3 = dgt * gt * (1.0 - gt)
    y = dz3 + f64(old)
    return y

@@ -1,0 +1,179 @@
+from contextlib import ExitStack
+
+import concourse.mybir as mybir
+
+F32 = mybir.dt.float32
+BF16 = mybir.dt.bfloat16
+I32 = mybir.dt.int32
+U32 = mybir.dt.uint32
+U8 = mybir.dt.uint8
+FP8X4 = mybir.dt.float8_e4m3fn_x4
+FP4X4 = mybir.dt.float4_e2m1fn_x4
+ACT = mybir.ActivationFunctionType
+ALU = mybir.AluOpType
+
+G, D, M, N = 2, 256, 256, 512
+P = 128
+ROWS = 64
+PACK = 4
+QUAD = 32
+FLOPS = 4 * 2 * G * D * M * N
+X_SCALAR_COLS = 192
+RUN = 4
+
+
+def tile_rows_bmixture_kernel(tc, x, w1_words, w1_scales, w2_words, w2_scales, w3_words, w3_scales, b3,
+                                  wo_words, wo_scales, dy, old, out):
+    nc = tc.nc
+    names = ("w2", "w1", "w3", "wo")
+    words_hbm = dict(zip(names, (w2_words, w1_words, w3_words, wo_words)))
+    scales_hbm = dict(zip(names, (w2_scales, w1_scales, w3_scales, wo_scales)))
+    tiles = [(g, h) for h in range(M // P) for g in range(G)]
+
+    with ExitStack() as ctx:
+        sb = ctx.enter_context(tc.tile_pool(name="sb", bufs=1))
+        ps = ctx.enter_context(tc.psum_pool(name="ps", bufs=1))
+        ctx.enter_context(tc.manual_schedule())
+
+        staged = sb.tile([P, PACK, len(names) * M // 4], I32, name="staged", align_bytes=64)
+        plane = sb.tile([P, len(names) * M], U8, name="plane", align_bytes=64)
+        words = {n: sb.tile([P, 2 * M], U8, name="words_" + n, align_bytes=64) for n in names}
+        raw = {n: sb.tile([P, PACK, N], F32, name="raw_" + n, align_bytes=64) for n in ("x", "dy")}
+        grouped = {n: sb.tile([P, N * PACK], BF16, name="grouped_" + n, align_bytes=64) for n in ("x", "dy")}
+        codes = {n: sb.tile([P, N], U32, name="codes_" + n, align_bytes=64) for n in ("x", "dy")}
+        scales = {n: sb.tile([P, N], U8, name="scales_" + n, align_bytes=64) for n in ("x", "dy")}
+        old_sb = sb.tile([P, G, M // P, N], F32, name="old_sb", align_bytes=64)
+        bias_rows = sb.tile([P, P], F32, name="bias_rows", align_bytes=64)
+        bias_turned = sb.tile([P, P], F32, name="bias_turned", align_bytes=64)
+        half_bias = sb.tile([P, len(tiles)], F32, name="half_bias", align_bytes=64)
+        warm_in = sb.tile([P, 1], F32, name="warm_in")
+        warm_out = sb.tile([P, 1], F32, name="warm_out")
+        work = {(kind, t): sb.tile([P, N], F32, name="%s_%d%d" % (kind, t[0], t[1]), align_bytes=64)
+                for kind in ("e1", "e2", "th", "sq", "diff", "u", "v", "y") for t in tiles}
+        bank = {(n, g): ps.tile([P, N], F32, name="bank_%s_%d" % (n, g)) for n in names for g in range(G)}
+
+        def stage_scales(queue, n):
+            i = names.index(n)
+            queue.dma_start(out=staged[0:P:QUAD, :, i * 64:(i + 1) * 64],
+                            in_=scales_hbm[n].rearrange("g (q r) m -> (g q) r m", r=PACK).bitcast(I32))
+
+        def load_words(queue, n):
+            queue.dma_start(out=words[n][:].bitcast(I32),
+                            in_=words_hbm[n].rearrange("g p b -> (g p) b").bitcast(I32))
+
+        def load_operand(n, hbm):
+            nc.sync.dma_start(out=raw[n][:], in_=hbm.rearrange("g (p j) c -> (g p) j c", j=PACK))
+
+        def interleave(copy, n, c0, c1):
+            dst = grouped[n][:, c0 * PACK:c1 * PACK].rearrange("p (c i j) -> p c j i", i=RUN, j=PACK)
+            src = raw[n][:, :, c0:c1].rearrange("p j (c i) -> p c j i", i=RUN)
+            copy(out=dst, in_=src)
+
+        def quantise(n, c0, c1):
+            nc.vector.quantize_mx(out=codes[n][:, c0:c1].bitcast(FP8X4), scales=scales[n][:, c0:c1],
+                                  in_=grouped[n][:, c0 * PACK:c1 * PACK])
+
+        def product(n, t):
+            g, h = t
+            rows = slice(g * ROWS, (g + 1) * ROWS)
+            operand = "dy" if n == "wo" else "x"
+            s0 = names.index(n) * M + h * P
+            nc.tensor.matmul_mx(out=bank[n, g][:],
+                                lhsT=words[n][rows, 2 * h * P:2 * (h + 1) * P].bitcast(FP4X4),
+                                lhsT_scale=plane[rows, s0:s0 + P],
+                                rhs=codes[operand][rows, :].bitcast(FP8X4),
+                                rhs_scale=scales[operand][rows, :], start=True, stop=True)
+
+        def activations(t):
+            g, h = t
+            col = g * (M // P) + h
+            nc.scalar.activation(out=work["e2", t][:], in_=bank["w2", g][:], func=ACT.Silu)
+            nc.scalar.activation(out=work["e1", t][:], in_=bank["w1", g][:], func=ACT.Tanh)
+            nc.scalar.activation(out=work["th", t][:], in_=bank["w3", g][:], func=ACT.Tanh,
+                                 bias=half_bias[:, col:col + 1], scale=0.5)
+            nc.scalar.activation(out=work["sq", t][:], in_=work["th", t][:], func=ACT.Square)
+
+        def step_diff(t):
+            nc.vector.tensor_tensor(out=work["diff", t][:], in0=work["e2", t][:], in1=work["e1", t][:], op=ALU.subtract)
+
+        def step_gate(t):
+            nc.vector.scalar_tensor_tensor(out=work["u", t][:], in0=work["sq", t][:], scalar=1.0, in1=bank["wo", t[0]][:],
+                                           op0=ALU.subtract, op1=ALU.mult)
+
+        def step_mix(t, cols):
+            nc.vector.scalar_tensor_tensor(out=work["v", t][:, cols], in0=work["u", t][:, cols], scalar=0.25,
+                                           in1=work["diff", t][:, cols], op0=ALU.mult, op1=ALU.mult)
+
+        def step_add(t, cols):
+            g, h = t
+            nc.vector.tensor_tensor(out=work["y", t][:, cols], in0=work["v", t][:, cols], in1=old_sb[:, g, h, cols], op=ALU.add)
+            nc.sync.dma_start(out=out[g, h * P:(h + 1) * P, cols], in_=work["y", t][:, cols])
+
+        def spread_scales(queue, r):
+            queue.dma_start(out=plane[r:P:QUAD, :].bitcast(I32), in_=staged[0:P:QUAD, r, :])
+
+        stage_scales(nc.sync, "w2")
+        stage_scales(nc.scalar, "w3")
+        stage_scales(nc.sync, "w1")
+        stage_scales(nc.scalar, "wo")
+        load_operand("x", x)
+        load_words(nc.sync, "w2")
+        load_words(nc.sync, "w1")
+        nc.vector.memset(warm_in[:], 0.0)
+        nc.vector.memset(bias_rows[:], 0.0)
+        nc.vector.memset(plane[:].bitcast(I32), 0)
+        nc.scalar.activation(out=warm_out[:], in_=warm_in[:], func=ACT.Silu)
+        load_words(nc.gpsimd, "w3")
+        nc.gpsimd.dma_start(out=bias_rows[0:P:QUAD, :].rearrange("q (t i) -> q t i", i=QUAD),
+                            in_=b3.rearrange("g (h q i) o -> q (g h) (i o)", q=P // QUAD, i=QUAD))
+        for r in range(PACK):
+            spread_scales(nc.sync if r < 2 else nc.scalar, r)
+        load_operand("dy", dy)
+        load_words(nc.sync, "wo")
+        nc.sync.dma_start(out=old_sb[:].rearrange("p g h c -> p (g h) c"),
+                          in_=old.rearrange("g (h p) c -> p (g h) c", p=P))
+
+        split = N - X_SCALAR_COLS
+        interleave(nc.scalar.copy, "x", split, N)
+        interleave(nc.vector.tensor_copy, "x", 0, N // 2)
+        interleave(nc.vector.tensor_copy, "x", N // 2, split)
+        quantise("x", 0, N // 2)
+        quantise("x", N // 2, N)
+        nc.vector.transpose(out=bias_turned[:], in_=bias_rows[:])
+        nc.vector.tensor_scalar(out=half_bias[:], in0=bias_turned[:, 0:P:QUAD], scalar1=0.5, scalar2=None, op0=ALU.mult)
+        interleave(nc.vector.tensor_copy, "dy", 0, N // 2)
+        interleave(nc.vector.tensor_copy, "dy", N // 2, N)
+        quantise("dy", 0, N // 2)
+        quantise("dy", N // 2, N)
+
+        t0, t1, t2, t3 = tiles
+        whole, left, right = slice(0, N), slice(0, N // 2), slice(N // 2, N)
+        for t in (t0, t1):
+            for n in ("w2", "w1", "w3"):
+                product(n, t)
+            activations(t)
+        product("wo", t0)
+        product("wo", t1)
+        step_diff(t0)
+        step_gate(t0)
+        step_diff(t1)
+        step_mix(t0, whole)
+        step_gate(t1)
+        for t in (t2, t3):
+            for n in ("w2", "w1", "w3"):
+                product(n, t)
+            activations(t)
+            product("wo", t)
+        step_add(t0, whole)
+        step_mix(t1, whole)
+        step_diff(t2)
+        step_add(t1, whole)
+        step_gate(t2)
+        step_diff(t3)
+        step_mix(t2, whole)
+        step_gate(t3)
+        step_add(t2, whole)
+        step_mix(t3, left)
+        step_mix(t3, right)
+        step_add(t3, left)
+        step_add(t3, right)

@@ -88,26 +88,28 @@ def tile_rows_bmixture_kernel(tc, x, w1_words, w1_scales, w2_words, w2_scales, w
             g, h = t
             col = g * (M // P) + h
             nc.scalar.activation(out=work["e2", t][:], in_=bank["w2", g][:], func=ACT.Silu)
-            nc.scalar.activation(out=work["e1", t][:], in_=bank["w1", g][:], func=ACT.Tanh)
             nc.scalar.activation(out=work["th", t][:], in_=bank["w3", g][:], func=ACT.Tanh,
                                  bias=half_bias[:, col:col + 1], scale=0.5)
+            nc.scalar.activation(out=work["e1", t][:], in_=bank["w1", g][:], func=ACT.Tanh)
             nc.scalar.activation(out=work["sq", t][:], in_=work["th", t][:], func=ACT.Square)
 
-        def step_diff(t):
-            nc.vector.tensor_tensor(out=work["diff", t][:], in0=work["e2", t][:], in1=work["e1", t][:], op=ALU.subtract)
-
-        def step_gate(t):
-            nc.vector.scalar_tensor_tensor(out=work["u", t][:], in0=work["sq", t][:], scalar=1.0, in1=bank["wo", t[0]][:],
-                                           op0=ALU.subtract, op1=ALU.mult)
-
-        def step_mix(t, cols):
-            nc.vector.scalar_tensor_tensor(out=work["v", t][:, cols], in0=work["u", t][:, cols], scalar=0.25,
-                                           in1=work["diff", t][:, cols], op0=ALU.mult, op1=ALU.mult)
-
-        def step_add(t, cols):
+        def combine(t, store_halves):
             g, h = t
-            nc.vector.tensor_tensor(out=work["y", t][:, cols], in0=work["v", t][:, cols], in1=old_sb[:, g, h, cols], op=ALU.add)
-            nc.sync.dma_start(out=out[g, h * P:(h + 1) * P, cols], in_=work["y", t][:, cols])
+            halves = (slice(0, N // 2), slice(N // 2, N))
+            nc.vector.tensor_tensor(out=work["diff", t][:], in0=work["e2", t][:], in1=work["e1", t][:], op=ALU.subtract)
+            for cols in halves:
+                nc.vector.scalar_tensor_tensor(out=work["u", t][:, cols], in0=work["sq", t][:, cols], scalar=1.0,
+                                               in1=bank["wo", g][:, cols], op0=ALU.subtract, op1=ALU.mult)
+            for cols in halves:
+                nc.vector.scalar_tensor_tensor(out=work["v", t][:, cols], in0=work["u", t][:, cols], scalar=0.25,
+                                               in1=work["diff", t][:, cols], op0=ALU.mult, op1=ALU.mult)
+            for cols in halves:
+                nc.vector.tensor_tensor(out=work["y", t][:, cols], in0=work["v", t][:, cols],
+                                        in1=old_sb[:, g, h, cols], op=ALU.add)
+                if store_halves:
+                    nc.sync.dma_start(out=out[g, h * P:(h + 1) * P, cols], in_=work["y", t][:, cols])
+            if not store_halves:
+                nc.sync.dma_start(out=out[g, h * P:(h + 1) * P, :], in_=work["y", t][:])
 
         def spread_scales(queue, r):
             queue.dma_start(out=plane[r:P:QUAD, :].bitcast(I32), in_=staged[0:P:QUAD, r, :])
@@ -116,19 +118,19 @@ def tile_rows_bmixture_kernel(tc, x, w1_words, w1_scales, w2_words, w2_scales, w
         stage_scales(nc.scalar, "w3")
         stage_scales(nc.sync, "w1")
         stage_scales(nc.scalar, "wo")
-        load_operand("x", x)
         load_words(nc.sync, "w2")
-        load_words(nc.sync, "w1")
+        load_words(nc.scalar, "w1")
+        load_words(nc.scalar, "w3")
+        load_operand("x", x)
         nc.vector.memset(warm_in[:], 0.0)
         nc.vector.memset(bias_rows[:], 0.0)
         nc.vector.memset(plane[:].bitcast(I32), 0)
         nc.scalar.activation(out=warm_out[:], in_=warm_in[:], func=ACT.Silu)
-        load_words(nc.gpsimd, "w3")
-        nc.gpsimd.dma_start(out=bias_rows[0:P:QUAD, :].rearrange("q (t i) -> q t i", i=QUAD),
-                            in_=b3.rearrange("g (h q i) o -> q (g h) (i o)", q=P // QUAD, i=QUAD))
         for r in range(PACK):
             spread_scales(nc.sync if r < 2 else nc.scalar, r)
         load_operand("dy", dy)
+        nc.scalar.dma_start(out=bias_rows[0:P:QUAD, :].rearrange("q (t i) -> q t i", i=QUAD),
+                            in_=b3.rearrange("g (h q i) o -> q (g h) (i o)", q=P // QUAD, i=QUAD))
         load_words(nc.sync, "wo")
         nc.sync.dma_start(out=old_sb[:].rearrange("p g h c -> p (g h) c"),
                           in_=old.rearrange("g (h p) c -> p (g h) c", p=P))
@@ -146,34 +148,14 @@ def tile_rows_bmixture_kernel(tc, x, w1_words, w1_scales, w2_words, w2_scales, w
         quantise("dy", 0, N // 2)
         quantise("dy", N // 2, N)
 
-        t0, t1, t2, t3 = tiles
-        whole, left, right = slice(0, N), slice(0, N // 2), slice(N // 2, N)
-        for t in (t0, t1):
-            for n in ("w2", "w1", "w3"):
-                product(n, t)
+        for k, t in enumerate(tiles):
+            product("w2", t)
+            product("w3", t)
+            if k > 0:
+                product("wo", tiles[k - 1])
+            product("w1", t)
             activations(t)
-        product("wo", t0)
-        product("wo", t1)
-        step_diff(t0)
-        step_gate(t0)
-        step_diff(t1)
-        step_mix(t0, whole)
-        step_gate(t1)
-        for t in (t2, t3):
-            for n in ("w2", "w1", "w3"):
-                product(n, t)
-            activations(t)
-            product("wo", t)
-        step_add(t0, whole)
-        step_mix(t1, whole)
-        step_diff(t2)
-        step_add(t1, whole)
-        step_gate(t2)
-        step_diff(t3)
-        step_mix(t2, whole)
-        step_gate(t3)
-        step_add(t2, whole)
-        step_mix(t3, left)
-        step_mix(t3, right)
-        step_add(t3, left)
-        step_add(t3, right)
+            if k > 0:
+                combine(tiles[k - 1], False)
+        product("wo", tiles[-1])
+        combine(tiles[-1], True)

@@ -19,6 +19,7 @@ PACK = 4
 QUAD = 32
 FLOPS = 4 * 2 * G * D * M * N
 X_SCALAR_COLS = 192
+DY_SCALAR_COLS = 64
 RUN = 4
 
 
@@ -119,40 +120,39 @@ def tile_rows_bmixture_kernel(tc, x, w1_words, w1_scales, w2_words, w2_scales, w
         stage_scales(nc.sync, "w1")
         stage_scales(nc.scalar, "wo")
         load_words(nc.sync, "w2")
-        load_words(nc.scalar, "w1")
-        load_words(nc.scalar, "w3")
         load_operand("x", x)
         nc.vector.memset(warm_in[:], 0.0)
         nc.vector.memset(bias_rows[:], 0.0)
         nc.vector.memset(plane[:].bitcast(I32), 0)
         nc.scalar.activation(out=warm_out[:], in_=warm_in[:], func=ACT.Silu)
-        for r in range(PACK):
-            spread_scales(nc.sync if r < 2 else nc.scalar, r)
-        load_operand("dy", dy)
         nc.scalar.dma_start(out=bias_rows[0:P:QUAD, :].rearrange("q (t i) -> q t i", i=QUAD),
                             in_=b3.rearrange("g (h q i) o -> q (g h) (i o)", q=P // QUAD, i=QUAD))
-        load_words(nc.sync, "wo")
+        for r in range(PACK):
+            spread_scales(nc.sync if r < PACK - 1 else nc.scalar, r)
+        load_operand("dy", dy)
+        for n in ("w3", "w1", "wo"):
+            load_words(nc.sync, n)
         nc.sync.dma_start(out=old_sb[:].rearrange("p g h c -> p (g h) c"),
                           in_=old.rearrange("g (h p) c -> p (g h) c", p=P))
 
-        split = N - X_SCALAR_COLS
-        interleave(nc.scalar.copy, "x", split, N)
-        interleave(nc.vector.tensor_copy, "x", 0, N // 2)
-        interleave(nc.vector.tensor_copy, "x", N // 2, split)
-        quantise("x", 0, N // 2)
-        quantise("x", N // 2, N)
+        def make_operand(n, scalar_cols):
+            split = N - scalar_cols
+            interleave(nc.scalar.copy, n, split, N)
+            interleave(nc.vector.tensor_copy, n, 0, N // 2)
+            interleave(nc.vector.tensor_copy, n, N // 2, split)
+            quantise(n, 0, N // 2)
+            quantise(n, N // 2, N)
+
+        make_operand("x", X_SCALAR_COLS)
         nc.vector.transpose(out=bias_turned[:], in_=bias_rows[:])
         nc.vector.tensor_scalar(out=half_bias[:], in0=bias_turned[:, 0:P:QUAD], scalar1=0.5, scalar2=None, op0=ALU.mult)
-        interleave(nc.vector.tensor_copy, "dy", 0, N // 2)
-        interleave(nc.vector.tensor_copy, "dy", N // 2, N)
-        quantise("dy", 0, N // 2)
-        quantise("dy", N // 2, N)
+        make_operand("dy", DY_SCALAR_COLS)
 
         for k, t in enumerate(tiles):
             product("w2", t)
-            product("w3", t)
             if k > 0:
                 product("wo", tiles[k - 1])
+            product("w3", t)
             product("w1", t)
             activations(t)
             if k > 0:

from contextlib import ExitStack

import concourse.mybir as mybir

F32 = mybir.dt.float32
BF16 = mybir.dt.bfloat16
I32 = mybir.dt.int32
U32 = mybir.dt.uint32
U8 = mybir.dt.uint8
FP8X4 = mybir.dt.float8_e4m3fn_x4
FP4X4 = mybir.dt.float4_e2m1fn_x4
ACT = mybir.ActivationFunctionType
ALU = mybir.AluOpType

G, D, M, N = 2, 256, 256, 512
P = 128
ROWS = 64
PACK = 4
QUAD = 32
FLOPS = 4 * 2 * G * D * M * N
X_SCALAR_COLS = 192
DY_SCALAR_COLS = 64
RUN = 4


def tile_rows_bmixture_kernel(tc, x, w1_words, w1_scales, w2_words, w2_scales, w3_words, w3_scales, b3,
                                  wo_words, wo_scales, dy, old, out):
    nc = tc.nc
    names = ("w2", "w1", "w3", "wo")
    words_hbm = dict(zip(names, (w2_words, w1_words, w3_words, wo_words)))
    scales_hbm = dict(zip(names, (w2_scales, w1_scales, w3_scales, wo_scales)))
    tiles = [(g, h) for h in range(M // P) for g in range(G)]

    with ExitStack() as ctx:
        sb = ctx.enter_context(tc.tile_pool(name="sb", bufs=1))
        ps = ctx.enter_context(tc.psum_pool(name="ps", bufs=1))
        ctx.enter_context(tc.manual_schedule())

        staged = sb.tile([P, PACK, len(names) * M // 4], I32, name="staged", align_bytes=64)
        plane = sb.tile([P, len(names) * M], U8, name="plane", align_bytes=64)
        words = {n: sb.tile([P, 2 * M], U8, name="words_" + n, align_bytes=64) for n in names}
        raw = {n: sb.tile([P, PACK, N], F32, name="raw_" + n, align_bytes=64) for n in ("x", "dy")}
        grouped = {n: sb.tile([P, N * PACK], BF16, name="grouped_" + n, align_bytes=64) for n in ("x", "dy")}
        codes = {n: sb.tile([P, N], U32, name="codes_" + n, align_bytes=64) for n in ("x", "dy")}
        scales = {n: sb.tile([P, N], U8, name="scales_" + n, align_bytes=64) for n in ("x", "dy")}
        old_sb = sb.tile([P, G, M // P, N], F32, name="old_sb", align_bytes=64)
        bias_rows = sb.tile([P, P], F32, name="bias_rows", align_bytes=64)
        bias_turned = sb.tile([P, P], F32, name="bias_turned", align_bytes=64)
        half_bias = sb.tile([P, len(tiles)], F32, name="half_bias", align_bytes=64)
        warm_in = sb.tile([P, 1], F32, name="warm_in")
        warm_out = sb.tile([P, 1], F32, name="warm_out")
        work = {(kind, t): sb.tile([P, N], F32, name="%s_%d%d" % (kind, t[0], t[1]), align_bytes=64)
                for kind in ("e1", "e2", "th", "sq", "diff", "u", "v", "y") for t in tiles}
        bank = {(n, g): ps.tile([P, N], F32, name="bank_%s_%d" % (n, g)) for n in names for g in range(G)}

        def stage_scales(queue, n):
            i = names.index(n)
            queue.dma_start(out=staged[0:P:QUAD, :, i * 64:(i + 1) * 64],
                            in_=scales_hbm[n].rearrange("g (q r) m -> (g q) r m", r=PACK).bitcast(I32))

        def load_words(queue, n):
            queue.dma_start(out=words[n][:].bitcast(I32),
                            in_=words_hbm[n].rearrange("g p b -> (g p) b").bitcast(I32))

        def load_operand(n, hbm):
            nc.sync.dma_start(out=raw[n][:], in_=hbm.rearrange("g (p j) c -> (g p) j c", j=PACK))

        def interleave(copy, n, c0, c1):
            dst = grouped[n][:, c0 * PACK:c1 * PACK].rearrange("p (c i j) -> p c j i", i=RUN, j=PACK)
            src = raw[n][:, :, c0:c1].rearrange("p j (c i) -> p c j i", i=RUN)
            copy(out=dst, in_=src)

        def quantise(n, c0, c1):
            nc.vector.quantize_mx(out=codes[n][:, c0:c1].bitcast(FP8X4), scales=scales[n][:, c0:c1],
                                  in_=grouped[n][:, c0 * PACK:c1 * PACK])

        def product(n, t):
            g, h = t
            rows = slice(g * ROWS, (g + 1) * ROWS)
            operand = "dy" if n == "wo" else "x"
            s0 = names.index(n) * M + h * P
            nc.tensor.matmul_mx(out=bank[n, g][:],
                                lhsT=words[n][rows, 2 * h * P:2 * (h + 1) * P].bitcast(FP4X4),
                                lhsT_scale=plane[rows, s0:s0 + P],
                                rhs=codes[operand][rows, :].bitcast(FP8X4),
                                rhs_scale=scales[operand][rows, :], start=True, stop=True)

        def activations(t):
            g, h = t
            col = g * (M // P) + h
            nc.scalar.activation(out=work["e2", t][:], in_=bank["w2", g][:], func=ACT.Silu)
            nc.scalar.activation(out=work["th", t][:], in_=bank["w3", g][:], func=ACT.Tanh,
                                 bias=half_bias[:, col:col + 1], scale=0.5)
            nc.scalar.activation(out=work["e1", t][:], in_=bank["w1", g][:], func=ACT.Tanh)
            nc.scalar.activation(out=work["sq", t][:], in_=work["th", t][:], func=ACT.Square)

        def combine(t, store_halves):
            g, h = t
            halves = (slice(0, N // 2), slice(N // 2, N))
            nc.vector.tensor_tensor(out=work["diff", t][:], in0=work["e2", t][:], in1=work["e1", t][:], op=ALU.subtract)
            for cols in halves:
                nc.vector.scalar_tensor_tensor(out=work["u", t][:, cols], in0=work["sq", t][:, cols], scalar=1.0,
                                               in1=bank["wo", g][:, cols], op0=ALU.subtract, op1=ALU.mult)
            for cols in halves:
                nc.vector.scalar_tensor_tensor(out=work["v", t][:, cols], in0=work["u", t][:, cols], scalar=0.25,
                                               in1=work["diff", t][:, cols], op0=ALU.mult, op1=ALU.mult)
            for cols in halves:
                nc.vector.tensor_tensor(out=work["y", t][:, cols], in0=work["v", t][:, cols],
                                        in1=old_sb[:, g, h, cols], op=ALU.add)
                if store_halves:
                    nc.sync.dma_start(out=out[g, h * P:(h + 1) * P, cols], in_=work["y", t][:, cols])
            if not store_halves:
                nc.sync.dma_start(out=out[g, h * P:(h + 1) * P, :], in_=work["y", t][:])

        def spread_scales(queue, r):
            queue.dma_start(out=plane[r:P:QUAD, :].bitcast(I32), in_=staged[0:P:QUAD, r, :])

        stage_scales(nc.sync, "w2")
        stage_scales(nc.scalar, "w3")
        stage_scales(nc.sync, "w1")
        stage_scales(nc.scalar, "wo")
        load_words(nc.sync, "w2")
        load_operand("x", x)
        nc.vector.memset(warm_in[:], 0.0)
        nc.vector.memset(bias_rows[:], 0.0)
        nc.vector.memset(plane[:].bitcast(I32), 0)
        nc.scalar.activation(out=warm_out[:], in_=warm_in[:], func=ACT.Silu)
        nc.scalar.dma_start(out=bias_rows[0:P:QUAD, :].rearrange("q (t i) -> q t i", i=QUAD),
                            in_=b3.rearrange("g (h q i) o -> q (g h) (i o)", q=P // QUAD, i=QUAD))
        for r in range(PACK):
            spread_scales(nc.sync if r < PACK - 1 else nc.scalar, r)
        load_operand("dy", dy)
        for n in ("w3", "w1", "wo"):
            load_words(nc.sync, n)
        nc.sync.dma_start(out=old_sb[:].rearrange("p g h c -> p (g h) c"),
                          in_=old.rearrange("g (h p) c -> p (g h) c", p=P))

        def make_operand(n, scalar_cols):
            split = N - scalar_cols
            interleave(nc.scalar.copy, n, split, N)
            interleave(nc.vector.tensor_copy, n, 0, N // 2)
            interleave(nc.vector.tensor_copy, n, N // 2, split)
            quantise(n, 0, N // 2)
            quantise(n, N // 2, N)

        make_operand("x", X_SCALAR_COLS)
        nc.vector.transpose(out=bias_turned[:], in_=bias_rows[:])
        nc.vector.tensor_scalar(out=half_bias[:], in0=bias_turned[:, 0:P:QUAD], scalar1=0.5, scalar2=None, op0=ALU.mult)
        make_operand("dy", DY_SCALAR_COLS)

        for k, t in enumerate(tiles):
            product("w2", t)
            if k > 0:
                product("wo", tiles[k - 1])
            product("w3", t)
            product("w1", t)
            activations(t)
            if k > 0:
                combine(tiles[k - 1], False)
        product("wo", tiles[-1])
        combine(tiles[-1], True)
